import numpy as np, ml_dtypes
CORES = [25,29,65,69,153,157,193,197]
N = 8
import mx_ref
BF = ml_dtypes.bfloat16
def gentries(a):
    return np.ascontiguousarray(a.reshape(8, 16, -1).transpose(0, 2, 1)).reshape(8, -1)
def gtable(e):
    e = np.asarray(e); return np.ascontiguousarray(e.reshape(8, -1, 16).transpose(0, 2, 1)).reshape(128, -1).astype(np.int32)
def gpick(z, e):
    return np.concatenate([z[16 * g:16 * g + 16][:, e[g]] for g in range(8)])
def cols(t, e):
    v = np.concatenate([t.reshape(128, -1, 4), np.zeros((128, 1, 4), BF)], axis=1)
    return np.ascontiguousarray(v[:, e]).reshape(128, -1)
def pick(q, e):
    c = np.concatenate([q[0].reshape(128, -1, 4), np.zeros((128, 1, 4), np.uint8)], axis=1); s = np.concatenate([q[1], np.ones((16, 1), np.uint8)], axis=1)
    return (np.ascontiguousarray(c[:, e].reshape(128, -1)), np.ascontiguousarray(s[:, e]))
def join(*qs):
    return (np.concatenate([q[0] for q in qs], axis=1), np.concatenate([q[1] for q in qs], axis=1))
def put(q, e, v):
    c, s = q[0].reshape(128, -1, 4).copy(), q[1].copy(); c[:, e] = v[0].reshape(128, -1, 4); s[:, e] = v[1]
    return (c.reshape(128, -1), s)
def pk(c, s):
    return (np.ascontiguousarray(c), mx_ref.live(s))
def emit(q):
    return q[0], q[1]
def values_of_codes():
    e, c = np.zeros((128, 128, 4), np.float32), np.zeros((128, 2, 4), np.uint8)
    e[np.arange(128), np.arange(128), 0] = 1
    c[:127, :, 0] = np.arange(256).reshape(2, 128).T[:127]
    return mx_ref.matmul(mx_ref.quantize(e.reshape(128, 512).astype(BF)), (c.reshape(128, 8), np.full((16, 2), 127, np.uint8))).T.reshape(-1).astype(np.float64)
CODE_VALUE, SCALE_VALUE = values_of_codes(), 2.0 ** (np.arange(256) - 127.0)
def decode(q):
    return (CODE_VALUE[q[0]].reshape(16, 8, -1, 4) * SCALE_VALUE[q[1]][:, None, :, None] + 0.0).reshape(128, -1).astype(np.float32)
def f(rng, *shape):
    return mx_ref.flush((rng.standard_normal(shape, dtype=np.float32) * np.exp2(rng.integers(-2, 3, shape[:-1] + (1,)))).astype(BF))
def wide(rng, *shape, cols=0):
    v = rng.standard_normal(shape, dtype=np.float32) * np.exp2(rng.integers(-12, 13, shape)).astype(np.float32)
    if cols: v *= np.repeat(np.exp2(rng.integers(-cols, cols + 1, shape[:-2] + (1, shape[-1] // 4))) * (rng.random(shape[:-2] + (1, shape[-1] // 4)) > 0.0625), 4, axis=-1).astype(np.float32)
    return mx_ref.flush(v.astype(BF))
T, S, CAPP, R = 3, 512, 16, 2
def coarse(v):
    v = v.astype(np.float32)
    v[np.abs(v) < np.float32(2.0 ** -16)] = 0
    return v.astype(BF)
def numbers_of(rng):
    return {"x": coarse(f(rng, N, 128, 512 * T)), "e": coarse(f(rng, N, 128, 4 * S)), "v": np.array(f(rng, N, 128, 512))}
def lists_of(rng):
    return {k: np.stack([gtable(rng.integers(0, S, (8, S))) for r in range(N)]) for k in ("pa", "pb")}
def signs(rng):
    return np.stack([rng.permutation(128) % 2 * 2.0 - 1.0 for r in range(N)]).astype(np.float32)
def setup_inputs(rng):
    return {**numbers_of(rng), **lists_of(rng)}
def setup_inputs_ties(rng):
    d = setup_inputs(rng)
    x = d["x"].reshape(N, 128, T, 128, 4)
    x[:, :, :, ::8] = 0
    for r in range(N):
        run = np.concatenate([rng.permutation(4), rng.permutation(4)])
        k = run[np.arange(S) * 8 // S]
        d["e"][r] = cols(d["e"][r], np.where(k == 3, -1, k))
        same = np.argsort(k, kind="stable").reshape(4, S // 4)
        a, b = gentries(d["pa"][r]), gentries(d["pb"][r])
        d["pb"][r] = gtable(np.where(rng.random((8, S)) < 0.5, same[k[a], rng.integers(0, S // 4, (8, S))], b))
    return {**d, "x": x.reshape(N, 128, 512 * T)}
def setup_inputs_near(rng):
    d = setup_inputs(rng)
    x = d["x"].reshape(N, 128, T, 128, 4)
    x[:, :96] = 0
    x[:, 0, :, :, 0] = signs(rng)[:, None, :].astype(BF)
    x[:, 8:10] = (rng.choice([-1.0, 1.0], (N, 2, T, 128, 4)) * 2.0 ** -4).astype(np.float32).astype(BF)
    e = d["e"].reshape(N, 128, S, 4)
    m = np.zeros((N, 128), bool)
    for r in range(N): m[r, 32 + 8 * r:40 + 8 * r] = True
    e[~m] = 0
    e[:, 0, :, 0] = 1
    s = np.arange(S) // 2
    g = (((s[:, None] >> np.arange(8)) & 1) * np.exp2(np.arange(8) - 19.0)).astype(np.float32).astype(BF)
    e[:, 8] = g[:, :4]
    e[:, 9] = g[:, 4:]
    for r in range(N):
        d["pb"][r] = gtable(gentries(d["pa"][r]) ^ rng.choice(np.array([1, 2, 2, 4]), (8, S)))
    small = np.float32(2.0 ** -8)
    return {**d, "x": (x.astype(np.float32) * small).astype(BF).reshape(N, 128, 512 * T), "e": (e.astype(np.float32) * small).astype(BF).reshape(N, 128, 4 * S)}
def setup_inputs_huge(rng):
    d = setup_inputs(rng)
    g = (rng.permutation(N) % 2 * 2.0 - 1.0) * 2.0 ** 26
    x = rng.integers(12, 16, (N, 128, T, 128, 4)) * 2.0 ** 26 * signs(rng)[:, None, None, :, None]
    e = rng.permuted(np.tile(np.arange(512) % 4 + 12, (N, S, 1)), axis=2).reshape(N, S, 128, 4).transpose(0, 2, 1, 3) * g[:, None, None, None]
    d["x"] = x.astype(np.float32).reshape(N, 128, 512 * T).astype(BF)
    d["e"] = np.ascontiguousarray(e.astype(np.float32)).reshape(N, 128, 4 * S).astype(BF)
    return d
def setup_inputs_crowd(rng):
    d = setup_inputs(rng)
    x = d["x"].reshape(N, 128, T, 128, 4)
    e = d["e"].reshape(N, 128, S, 4)
    x[:, 0:8 * N:8] = 0
    e[:, 0:8 * N:8] = 0
    e[:, np.arange(S) // (S // N) * 8, np.arange(S), 0] = 1024
    o = rng.permutation(N)
    rest = np.array([c for c in o if c not in (o[0], o[1], o[3])])
    for r in range(N):
        to = np.full(128, o[1])
        if r != o[0] and r != o[1]:
            to[:CAPP] = o[0]
            to[2 * CAPP + 1:] = np.resize(rest, 128 - 2 * CAPP - 1)
        to = rng.permutation(to)
        x[r, 8 * to, T - 1, np.arange(128), 0] = 4096
    return {**d, "x": x.reshape(N, 128, 512 * T), "e": e.reshape(N, 128, 4 * S)}
def setup_inputs_spread(rng):
    d = setup_inputs(rng)
    d["x"] = coarse(wide(rng, N, 128, 512 * T, cols=6))
    d["e"] = coarse(wide(rng, N, 128, 4 * S))
    return d
def check_inputs(d):
    b = []
    for k in ("x", "e", "v"):
        a = np.abs(d[k].astype(np.float32))
        if not (np.isfinite(a).all() and ((a == 0) | (a >= 2.0 ** -30) & (a <= 2.0 ** 30)).all()): b.append("a value of " + k)
    for k in ("pa", "pb"):
        if not ((d[k] >= 0) & (d[k] < S)).all(): b.append("an entry of " + k)
    return b
def trace(q, w, a, b):
    p = np.arange(128)
    s = mx_ref.matmul(pick(q, p), w)
    came = []
    for t in range(1, T):
        m, n = gpick(s, a), gpick(s, b)
        came.append(np.where(n > m, np.repeat(b, 16, axis=0), np.repeat(a, 16, axis=0)))
        s = np.maximum(m, n) + mx_ref.matmul(pick(q, 128 * t + p), w)
    path = np.zeros((128, T), int)
    path[:, T - 1] = np.argmax(s + np.float32(0.0), axis=1)
    for t in range(T - 1, 0, -1): path[:, t - 1] = came[t - 1][p, path[:, t]]
    return path
def reference(x, e, v, pa, pb):
    a, b = [gentries(pa[r]) for r in range(N)], [gentries(pb[r]) for r in range(N)]
    qe = [mx_ref.quantize(e[r]) for r in range(N)]
    data = join(*[mx_ref.quantize(x[r]) for r in range(N)])
    mine = [128 * T * r + np.arange(128 * T) for r in range(N)]
    for turn in range(R):
        home = [trace(pick(data, mine[r]), qe[r], a[r], b[r]) for r in range(N)]
        visit, at, new = [], [], []
        for c in range(N):
            slot = np.full((T, 128), -1)
            for r in range(N):
                p = np.flatnonzero(home[r][:, T - 1] // (S // N) == c)[:CAPP]
                slot[:, CAPP * r:CAPP * r + len(p)] = 128 * T * r + 128 * np.arange(T)[:, None] + p
            slot = slot.reshape(-1)
            q = pick(data, slot)
            path = trace(q, qe[c], a[c], b[c])
            z = (decode(q) + decode(pick(qe[c], path.transpose().reshape(-1)))) * np.float32(0.5)
            full = np.flatnonzero(slot >= 0)
            at.append(slot[full])
            new.append(pick(mx_ref.quantize(np.ascontiguousarray(z.astype(BF))), full))
            visit.append(path)
        data = put(data, np.concatenate(at), join(*new))
    y, ol, dl = np.zeros((N, 128, 128 * T), np.float32), np.zeros((N, 128, T), np.float32), np.zeros((N, N * CAPP, T), np.float32)
    oc, osc = np.zeros((N, 128, 512 * T), np.uint8), np.zeros((N, 16, 128 * T), np.uint8)
    for r in range(N):
        q = pick(data, mine[r])
        y[r] = mx_ref.matmul(mx_ref.quantize(v[r]), q)
        ol[r] = home[r]
        dl[r] = visit[r][:N * CAPP]
        oc[r], osc[r] = emit(q)
    return {"y": y, "ol": ol, "dl": dl, "oc": oc, "osc": osc}

from concourse.bass import DstId, RemoteDMATransfer
from concourse.mybir import dt, AluOpType, AxisListType, ActivationFunctionType

ALU = AluOpType
ACT = ActivationFunctionType
N, TT, S, CAP = 8, 3, 512, 16
SIM_CORES = 256
BLK = TT * CAP
ALL = N * BLK
HALF = ALL // 2
XS = 144
XW = TT * XS
Q4, U8 = "float8_e4m3fn_x4", "uint8"

SCRATCH = {"zf": ("sbuf", [128, 8, 32], "float32"), "zo": ("sbuf", [128, 8, 32], "float32"),
           "ps": ("psum", [128, 4096], "float32")}
for _d, _l in (("bfloat16", (("xt", 4 * XW), ("et", 4 * S), ("vt", 512), ("ones", 2048), ("unit", 2048), ("ntab", 32),
                             ("tri", 128), ("ib", 32), ("rw", 128), ("rf", 128), ("eq", 128), ("eq2", 128),
                             ("cum", 128), ("jb", 256), ("bl1", 4 * ALL), ("bl2", 4 * ALL))),
               ("int32", (("pai", 32), ("pbi", 32), ("pi", 4), ("pj", 4))),
               ("uint16", (("au", 32), ("bu", 32), ("su", 8), ("ls", 24), ("lf1", 24), ("lf2", 24), ("lp1", 24),
                           ("lp2", 24), ("lr1", 32), ("lr2", 32))),
               ("float32", (("iot", 512), ("cst", 256), ("sm", 512), ("jk", 1024), ("inF", 32), ("inP", 32),
                            ("inH", 32), ("inR", 32), ("zr", 128), ("da", 5120), ("db", 5120), ("yt", 384)))):
    for _n, _w in _l:
        SCRATCH[_n] = ("sbuf", [128, _w], _d)
for _n, _w in ([("e", S), ("v", 128), ("u", 512), ("x1", XW), ("x2", XW), ("x3", ALL)]
               + [("%s%d" % (_a, _r), _b) for _r in (1, 2)
                  for _a, _b in (("ex", 2 * ALL), ("sl", ALL), ("rt", 2 * ALL - BLK), ("w", XW + ALL))]
               + [("rl%d" % _x, 2 * BLK) for _x in range(4)]):
    SCRATCH[_n + "C"] = ("sbuf", [128, _w], Q4)
    SCRATCH[_n + "S"] = ("sbuf", [128, _w], U8)

SEMAPHORES = (["cv", "cs", "cp", "cg", "snt"] + ["%s%d" % (_a, _x) for _a in "abr" for _x in range(4)]
              + ["d%d" % _k for _k in range(24)])


def layout(cores, topo):
    def place(c):
        return (topo.host(c), topo.chip(c))
    L = []
    for r in range(N):
        c = cores[r]
        peer = [s for s in range(N) if s != r and place(cores[s]) == place(c)]
        near = [s for s in range(N) if place(cores[s]) != place(c) and topo.may_write(c, cores[s])]
        far = [s for s in range(N) if not topo.may_write(c, cores[s])]
        fx = [s for s in far if topo.host(cores[s]) == topo.host(c)]
        fy = [s for s in far if s not in fx]
        assert len(peer) == 1 and peer[0] // 2 == r // 2
        for pr in (near, fx, fy):
            assert len(pr) == 2 and pr[0] % 2 == 0 and pr[1] == pr[0] + 1
        rx = [k for k in topo.cores_of(c) if k not in cores and topo.die(k) == topo.die(c)
              and topo.may_write(k, cores[fx[0]])]
        ry = [k for k in range(SIM_CORES) if topo.mates(k, cores[fy[0]]) and topo.die(k) == topo.die(c)
              and topo.may_write(k, cores[fy[0]]) and topo.may_write(c, k)]
        low = r < peer[0]
        if low:
            fo = fx[::-1] + fy[::-1] + near[::-1] + [peer[0], r]
            so = [r, peer[0]] + near + fx + fy
        else:
            fo = [r, peer[0]] + near[::-1] + fx[::-1] + fy[::-1]
            so = fy + fx + near + [peer[0], r]
        L.append({"peer": peer[0], "near": near, "fx": fx, "fy": fy, "rx": rx[:2], "ry": ry[:2], "fo": fo, "so": so,
                  "land": 0 if low else ALL - BLK, "send": ALL - BLK if low else 0})
    return L


def landing(L, x, src, dst):
    rnd = x // 2 + 1
    if x % 2 == 0:
        return "ex%d" % rnd, ALL + BLK * src
    return "rt%d" % rnd, L[dst]["land"] + BLK * L[dst]["fo"].index(src)


def wire(T, name, a, b):
    ap = T[name][:, a:b]
    return ap.bitcast(dt.uint8) if name.endswith("C") else ap


def transfer(T, topo, me, to, engines, sem, src, dst):
    rid, pid = topo.addr(to, me)
    return RemoteDMATransfer(dst_ids=[DstId(rid=rid, pnc=pid)], dma_engine_mask=sum(1 << e for e in engines),
                             remote_sem=T.sem[sem], src=src, dst=dst)


def arrival_sem(x, kind, far):
    if x % 2 == 0:
        return ("a%d" if kind == "C" else "b%d") % x
    return ("b%d" if far else "a%d") % x


def relay_program(g, core, T, topo, L, src, kind, pair):
    cores = list(T.cores)
    eng = topo.engines(core, cores[pair[0]])
    half = len(eng) // 2
    got = len(topo.engines(cores[src], cores[L[src]["near"][0]]))
    for x in range(4):
        g.wait_ge(T.sem["r%d" % x], got)
        order = [d for d in (L[src]["fo"] if x % 2 == 0 else L[src]["so"]) if d in pair]
        tr = []
        for k, d in enumerate(order):
            stem, c0 = landing(L, x, src, d)
            tr.append(transfer(T, topo, core, cores[d], eng[k * half:(k + 1) * half], arrival_sem(x, kind, True),
                               wire(T, "rl%d%s" % (x, kind), k * BLK, (k + 1) * BLK),
                               wire(T, stem + kind, c0, c0 + BLK)))
        g.remote_dma_fused(tr, local_sem=T.sem.snt)
    g.wait_ge(T.sem.snt, 4 * 2 * half)


def rank_program(g, core, T, topo):
    cores = list(T.cores)
    L = layout(cores, topo)
    rank = T.rank_of(core)
    if rank is None:
        for r in range(N):
            for key, pair in (("rx", "fx"), ("ry", "fy")):
                if core in L[r][key]:
                    relay_program(g, core, T, topo, L, r, "CS"[L[r][key].index(core)], L[r][pair])
        return
    me = L[rank]
    fo, so = me["fo"], me["so"]

    Qs = {"V": g.vector, "S": g.scalar, "P": g.tensor, "G": g, "Y": g.sync}
    own = {"V": "cv", "S": "cs", "P": "cp", "G": "cg"}
    count = {"cv": 0, "cs": 0, "cp": 0, "cg": 0}
    known = {q: {} for q in Qs}
    log = {}
    final = {}
    waited = {}
    ndma = [0]

    def v(name, c0, c1, step=1, p0=0, p1=128):
        ap = T[name][p0:p1, c0:c1] if step == 1 else T[name][p0:p1, c0:c1:step]
        return (ap, [(name, p0, p1, c0, c1, step)])

    def vq(name, c0, c1, a, n=1):
        return v(name, c0, c1, 1, 32 * a, 32 * (a + n))

    def v3(name, h0, h1, c0, c1, p0=0, p1=32, one=False):
        ap = T[name][p0:p1, h0:h1, c0] if one else T[name][p0:p1, h0:h1, c0:c1]
        return (ap, [(name, p0, p1, 32 * h + c0, 32 * h + c1, 1) for h in range(h0, h1)])

    def bank(b, n):
        return (T.ps[:, 512 * b:512 * b + n], [("ps", 0, 128, 512 * b, 512 * b + 512, 1)])

    def ind(win, off):
        return (win[0].indirect(off[0]), win[1] + off[1])

    def meets(a, b):
        if a[1] >= b[2] or b[1] >= a[2] or a[3] >= b[4] or b[3] >= a[4]:
            return False
        return not (a[5] > 1 and a[5] == b[5] and (a[3] - b[3]) % a[5] != 0)

    def wait(q, tok):
        if known[q].get(tok[0], 0) < tok[1]:
            Qs[q].wait_ge(T.sem[tok[0]], tok[1])
            waited[tok[0]] = max(waited.get(tok[0], 0), tok[1])
            known[q][tok[0]] = tok[1]
            for k, n in tok[2].items():
                if known[q].get(k, 0) < n:
                    known[q][k] = n

    def marks(reads, writes):
        return [(f, False) for r in reads for f in r[1]] + [(f, True) for w in writes for f in w[1]]

    def before(q, reads, writes):
        need = []
        for fp, wr in marks(reads, writes):
            for (f2, w2, q2, tok) in log.get(fp[0], []):
                if meets(fp, f2) and (q != q2 if fp[0] == "ps" else wr or w2):
                    need.append(tok)
        need.sort(key=lambda t: -t[1])
        for tok in need:
            wait(q, tok)

    def after(q, reads, writes, tok):
        for fp, wr in marks(reads, writes):
            log.setdefault(fp[0], []).append((fp, wr, q, tok))
        final[tok[0]] = max(final.get(tok[0], 0), tok[1])

    def op(q, make, reads, writes):
        before(q, reads, writes)
        s = own[q]
        count[s] += 1
        make().then_inc(T.sem[s], 1)
        after(q, reads, writes, (s, count[s], dict(known[q])))

    def dma(q, out, in_, reads, writes):
        before(q, reads, writes)
        s = "d%d" % ndma[0]
        ndma[0] += 1
        Qs[q].dma_start(out, in_).then_inc(T.sem[s], 16)
        after(q, reads, writes, (s, 16, dict(known[q])))

    def aps(*xs):
        return [x for x in xs if isinstance(x, tuple)]

    def val(x):
        return x[0] if isinstance(x, tuple) else x

    def copy(out, in_):
        op("V", lambda: g.vector.tensor_copy(out[0], in_[0]), [in_], [out])

    def tt(out, a, b, alu):
        op("V", lambda: g.vector.tensor_tensor(out[0], a[0], b[0], alu), [a, b], [out])

    def ts(out, a, s1, op0, s2=None, op1=None):
        if op1 is None:
            op("V", lambda: g.vector.tensor_scalar(out[0], a[0], val(s1), None, op0), aps(a, s1), [out])
        else:
            op("V", lambda: g.vector.tensor_scalar(out[0], a[0], val(s1), val(s2), op0, op1), aps(a, s1, s2), [out])

    def memset(out, c):
        op("V", lambda: g.vector.memset(out[0], c), [], [out])

    def red(out, in_):
        op("V", lambda: g.vector.tensor_reduce(out[0], in_[0], AxisListType.X, ALU.add), [in_], [out])

    def turn(out, in_):
        op("V", lambda: g.vector.transpose(out[0], in_[0]), [in_], [out])

    def scan(out, a, b, init, op0, op1):
        op("V", lambda: g.vector.tensor_tensor_scan(out[0], a[0], b[0], val(init), op0, op1), aps(a, b, init), [out])

    def scopy(out, in_, scale=None):
        if scale is None:
            op("S", lambda: g.scalar.activation(out[0], in_[0], ACT.Copy), [in_], [out])
        else:
            op("S", lambda: g.scalar.activation(out[0], in_[0], ACT.Copy, scale=scale), [in_], [out])

    def below(junk, in_, top, acc):
        op("S", lambda: g.scalar.activation(junk[0], in_[0], ACT.Sign, bias=top[0], scale=-1.0, accum_out=acc[0]),
           [in_, top], [junk, acc])

    def quant(stem, c0, c1, tile):
        op("V", lambda: g.vector.quantize_mx(T[stem + "C"][:, c0:c1], T[stem + "S"][:, c0:c1], tile[0]),
           [tile], [v(stem + "C", c0, c1), v(stem + "S", c0, c1)])

    def mm(b, w, w0, x, x0, n, start=True, stop=True):
        r = [v(w + "C", w0, w0 + 128), v(w + "S", w0, w0 + 128), v(x + "C", x0, x0 + n), v(x + "S", x0, x0 + n)]
        op("P", lambda: g.tensor.matmul_mx(bank(b, n)[0], r[0][0], r[1][0], r[2][0], r[3][0], start, stop),
           r, [bank(b, n)])

    def pick(dst, c0, src, width, lst, a, b):
        off, n = v(lst, a, b), 16 * (b - a)
        o, w = v(dst + "C", c0, c0 + n), v(src + "C", 0, width)
        op("V", lambda: g.vector.tensor_copy(o[0].bitcast(dt.uint32), w[0].bitcast(dt.uint32).indirect(off[0])),
           [w, off], [o])
        scopy(v(dst + "S", c0, c0 + n), ind(v(src + "S", 0, width), off))

    def iota(out, pattern, base, cm, whole=False):
        if whole:
            op("G", lambda: g.iota(out[0], pattern, base, cm), [], [out])
        else:
            op("G", lambda: g.iota(out[0], pattern, base, cm, allow_small_or_imprecise_dtypes=True), [], [out])

    pm16, rhalf, hb, pcol = v("cst", 0, 1), v("cst", 1, 2), v("cst", 2, 3), v("cst", 4, 5)
    otab, tabd, tab2 = v("cst", 4, 7), v("cst", 8, 11), v("cst", 12, 15)
    ktab, lsf = v("cst", 16, 24), v("cst", 64, 88)
    rows = {2: v("cst", 96, 100), 1: v("cst", 100, 104)}
    diag4, keep = v("cst", 128, 192), v("cst", 192, 256)
    dest, cnt, destm, cpos, kpos, adm, xpos = [v("sm", k, k + 1) for k in range(7)]
    A0, A1, A2, PM, K2, H2, AF, DF, K1, H1 = [512 * k for k in range(10)]

    def load(q, name, c0, src, s0, n):
        dma(q, T[name][:, c0:c0 + n], T[src][:, s0:s0 + n], [], [v(name, c0, c0 + n)])
    load("S", "et", 0, "e", 0, 1024)
    load("Y", "xt", 0, "x", 0, 512)
    load("S", "et", 1024, "e", 1024, 1024)
    load("Y", "pai", 0, "pa", 0, 32)
    load("S", "pbi", 0, "pb", 0, 32)
    load("Y", "xt", 4 * XS, "x", 512, 512)
    load("Y", "xt", 8 * XS, "x", 1024, 512)
    load("Y", "vt", 0, "v", 0, 512)

    iota(v("pi", 0, 1), [[0, 1]], 0, 1, True)
    iota(tab2, [[2 * XS, 3]], 128, 0)
    iota(v("iot", 0, 512), [[1, 512]], 0, 0)
    iota(otab, [[XS, 3]], 0, 1)
    iota(tabd, [[CAP - XS, 3]], XW, -1)
    iota(lsf, [[CAP, 3], [BLK, 8]], ALL, 0)
    for t in range(TT):
        memset(v("xt", 4 * XS * t + 512, 4 * XS * (t + 1)), 0.0)
    memset(v("ones", 0, 2048), 1.0)
    op("G", lambda: g.affine_select(T.unit[:], T.ones[:], [[-1, 4], [-8, 128], [1, 4]], ALU.is_equal, 0.0, 0, 8),
       [v("ones", 0, 2048)], [v("unit", 0, 2048)])
    memset(v("ntab", 0, 16), -1.0)
    memset(v("ntab", 16, 32), 0.0)
    for n in ("inF", "inP", "inH", "inR"):
        memset(v(n, 0, 32), 0.0)
    memset(keep, 1.0)
    for d in range(N):
        memset(v("cst", 16 + d, 17 + d), float(BLK * fo.index(d)))
    for r in (1, 2):
        memset(v("lr%d" % r, 0, 32), 128)
    ts(v("pj", 0, 1), v("pi", 0, 1), 15, ALU.bitwise_and)
    ts(v("pj", 1, 2), v("pi", 0, 1), 4, ALU.logical_shift_right, 1, ALU.bitwise_and)
    copy(pm16, v("pj", 0, 1))
    copy(hb, v("pj", 1, 2))
    ts(rhalf, pm16, 0.5, ALU.add)

    def later_constants():
        af = v("da", AF, AF + 512)
        scopy(af, ind(v("iot", 0, 512), v("au", 0, 32)))
        mine = v("cst", 64 + rank, 88, 8)
        ts(mine, mine, float(BLK * fo.index(rank) - ALL - BLK * rank), ALU.add)
        quant("u", 0, 512, v("unit", 0, 2048))
        ts(v("ls", 0, 24), lsf, pm16, ALU.add)
        for k in range(4):
            ts(v("cst", 128 + 16 * k, 144 + 16 * k), v("iot", 0, 16), pm16, ALU.is_equal)
        ts(rows[2], v("iot", 0, 4), 512.0, ALU.mult)
        ts(v("cst", 100, 102), v("iot", 2, 4), 512.0, ALU.mult)
        ts(v("cst", 102, 104), v("iot", 0, 2), 512.0, ALU.mult)
        ts(v("cst", 192, 256, 16), v("iot", 0, 4), 0.0, ALU.mult)
        ts(v("tri", 0, 128), v("iot", 0, 128), pcol, ALU.is_lt)
        tt(v("da", DF, DF + 512), ind(v("iot", 0, 512), v("bu", 0, 32)), af, ALU.subtract)
        quant("v", 0, 128, v("vt", 0, 512))
        dma("Y", T.db[:, AF:AF + 1024], T.da[:, AF:AF + 1024], [v("da", AF, AF + 1024)], [v("db", AF, AF + 1024)])

    CH = ((0, 128), (128, 320), (320, 512))

    def gath_s(D, dst, src, lst, a, b):
        scopy(v(D, dst + a, dst + b), ind(v(D, src, src + 512), v(lst, a // 16, b // 16)))

    def step(D, src, K, dst, b, hook=None):
        win = v(D, src, src + 512)

        def larger(c):
            tt(v(D, dst + c[0], dst + c[1]), ind(win, v("au", c[0] // 16, c[1] // 16)), v(D, K + c[0], K + c[1]), ALU.max)

        def plus(c):
            f = (T.ps[:, 512 * b + c[0]:512 * b + c[1]], bank(b, 512)[1])
            tt(v(D, dst + c[0], dst + c[1]), v(D, dst + c[0], dst + c[1]), f, ALU.add)
        gath_s(D, K, src, "bu", CH[1][0], CH[1][1])
        gath_s(D, K, src, "bu", CH[2][0], CH[2][1])
        copy(v(D, K, K + CH[0][1]), ind(win, v("bu", 0, CH[0][1] // 16)))
        larger(CH[0])
        if hook:
            hook()
        larger(CH[1])
        if hook:
            larger(CH[2])
        plus(CH[0])
        if not hook:
            larger(CH[2])
        plus(CH[1])
        plus(CH[2])

    def decode(D, X, stride, paths, make, late):
        def second():
            make(2)
            mm(2, X, stride, "e", 0, 512)
        make(0)
        mm(0, X, 0, "e", 0, 256)
        mm(1, X, 0, "e", 256, 256)
        make(1)
        copy(v(D, A0, A0 + 256), bank(0, 256))
        scopy(v(D, A0 + 256, A0 + 512), bank(1, 256))
        if not late:
            second()
        step(D, A0, K1, A1, 2, second if late else None)
        make(3)
        mm(3, X, 2 * stride, "e", 0, 512)
        if paths:
            gath_s(D, H1, A0, "au", 0, 192)
        step(D, A1, K2, A2, 3)
        if paths:
            gath_s(D, H2, A1, "au", 0, 512)
            gath_s(D, H1, A0, "au", 192, 512)
        a2 = v(D, A2, A2 + 512)
        scan(v(D, PM, PM + 512), a2, a2, v(D, A2, A2 + 1), ALU.max, ALU.max)

    CUT = 352

    def back(D, In):
        top = v(D, PM + 511, PM + 512)
        s1, s2 = v("sm", 8, 9), v("sm", 9, 10)
        below(v("jk", 0, CUT), v(D, PM, PM + CUT), top, s1)
        ts(v("jb", 0, 512 - CUT), v(D, PM + CUT, PM + 512), top, ALU.is_lt)
        red(s2, v("jb", 0, 512 - CUT))
        for t, w0 in ((2, K2), (1, AF)):
            off = v("su", 4 * t - 4, 4 * t)
            c0 = 128 * t
            got, run = v("sm", c0, c0 + 64), v("sm", c0 + 64, c0 + 128)
            ts(off, rows[t], s1, ALU.add, s2, ALU.add)
            tt(v(In, t, t + 1), s1, s2, ALU.add)
            tt(got, ind(v(D, w0, w0 + 2048), off), diag4, ALU.mult)
            scan(run, keep, got, 0.0, ALU.mult, ALU.add)
            k, h, a, d = [v("sm", c0 + 79 + 16 * j, c0 + 80 + 16 * j) for j in range(4)]
            s1, s2 = a, v("sm", 10 + t, 11 + t)
            ts(s2, k, h, ALU.is_gt, d, ALU.mult)
        tt(v(In, 0, 1), s1, s2, ALU.add)

    def spread(In, first, runs):
        turn(vq("zr", 0, 32, 0, 2), vq(In, 0, 32, 2 * first, 2))
        turn(vq("zr", 32, 64, 0, 2), vq(In, 0, 32, 2 - 2 * first, 2))
        (q0, h0), (q1, h1) = runs
        for d in range(2):
            copy(v3("zf", h0, h0 + 4, 16 * d, 16 * d + 16), vq("zr", 0, 64, q0))
            scopy(v3("zf", h0, h0 + 4, 16 * d, 16 * d + 16, 32, 64), vq("zr", 0, 64, q0))
        for p in (0, 32):
            for d in range(2):
                scopy(v3("zf", h1, h1 + 4, 16 * d, 16 * d + 16, p, p + 32), vq("zr", 0, 64, q1))

    kfar = fo.index(me["fx"][0]) // 4 * 4
    quarter = [kfar, 4 - kfar, kfar + 2, 6 - kfar]

    def slot_list(D):
        below(v("jk", 512, 520), v(D, PM + 63, PM + 512, 64), v(D, PM + 511, PM + 512), dest)
        ts(v("ib", 0, 32), v("ntab", 0, 32), dest, ALU.add)
        for a in range(4):
            turn(vq("rw", 32 * a, 32 * a + 32, 0), vq("ib", 0, 32, a))
        for a in range(4):
            ts(vq("eq", 0, 128, a), vq("rw", 0, 128, 0), float(fo[quarter[a] + 1]), ALU.is_equal)
        scan(v("cum", 0, 128), v("eq", 0, 128), v("eq", 0, 128), 0.0, ALU.add, ALU.max)
        below(v("jk", 640, 768), v("cum", 0, 128), rhalf, cnt)
        ts(v("inF", 0, 3), tab2, cnt, ALU.add, 0.5, ALU.mult)
        spread("inF", 0, ((0, kfar), (1, 4 - kfar)))

    def home_list(lst, at):
        for a in range(4):
            copy(vq("rf", 0, 128, a), vq("rw", 0, 128, 0))
        ts(destm, dest, hb, ALU.add, -1.0, ALU.add)
        ts(v("sm", 16, 24), v("iot", 0, 8), dest, ALU.is_equal)
        ts(v("eq2", 0, 128), v("rf", 0, 128), destm, ALU.is_equal)
        tt(v("sm", 24, 32), v("sm", 16, 24), ktab, ALU.mult)
        tt(v("rf", 0, 128), v("eq2", 0, 128), v("tri", 0, 128), ALU.mult)
        red(kpos, v("sm", 24, 32))
        red(cpos, v("rf", 0, 128))
        ts(adm, cpos, float(CAP), ALU.is_lt)
        tt(xpos, cpos, kpos, ALU.add)
        ts(v("sm", 32, 35), tabd, xpos, ALU.add, adm, ALU.mult)
        tt(v("inR", 0, 3), v("sm", 32, 35), otab, ALU.add)
        for a in range(4):
            turn(vq("zr", 32 * a, 32 * a + 32, 0), vq("inR", 0, 32, a))
        for d in range(2):
            copy(v3("zf", 0, 8, 16 * d, 16 * d + 16), vq("zr", 0, 128, 0))
        turn(v3("zo", 0, 8, 0, 32), v3("zf", 0, 8, 0, 32))
        for t in range(TT):
            copy(vq(lst, at[t], at[t] + 8, 0), v3("zo", 0, 8, t, t + 1, 0, 32, True))
        for a in range(1, 4):
            copy(vq(lst, 0, 32, a), vq(lst, 0, 32, 0))

    off_eng = topo.engines(core, cores[me["near"][0]])
    on_eng = [e for e in topo.engines(core, cores[me["peer"]]) if e not in off_eng]
    half = len(off_eng) // 2
    sent = [0]

    def exchange(x, stem, base, order, src, width, lst):
        kf = order.index(me["fx"][0]) // 4 * 4
        kn = 4 - kf
        cx, cy = [base + BLK * (order.index(me[f][0]) // 2 * 2) for f in ("fx", "fy")]
        for k in (kf, kn):
            turn(v3("zo", k, k + 4, 0, 32, 0, 64), v3("zf", k, k + 4, 0, 32, 0, 64))
            for a in (0, 2):
                copy(vq(lst, 3 * k, 3 * k + 12, a, 2), v3("zo", k, k + 4, 0, 3, 0, 64))
            pick(stem, base + BLK * k, src, width, lst, 3 * k, 3 * k + 12)
        for j, kind in enumerate("CS"):
            n = stem + kind
            before("G", [v(n, base + BLK * kf, base + BLK * kf + HALF)], [])
            rl = wire(T, "rl%d%s" % (x, kind), 0, 2 * BLK)
            g.remote_dma_fused([transfer(T, topo, core, me["rx"][j], on_eng, "r%d" % x, wire(T, n, cx, cx + 2 * BLK), rl),
                                transfer(T, topo, core, me["ry"][j], off_eng, "r%d" % x, wire(T, n, cy, cy + 2 * BLK), rl)],
                               local_sem=T.sem.snt)
            sent[0] += len(on_eng) + len(off_eng)
        for kind in "CS":
            n = stem + kind
            before("G", [v(n, base + BLK * kn, base + BLK * kn + HALF)], [])
            tr = []
            for d, eng in ((me["near"][0], off_eng[:half]), (me["near"][1], off_eng[half:]), (me["peer"], on_eng)):
                s0 = base + BLK * order.index(d)
                st, l0 = landing(L, x, rank, d)
                tr.append(transfer(T, topo, core, cores[d], eng, arrival_sem(x, kind, False),
                                   wire(T, n, s0, s0 + BLK), wire(T, st + kind, l0, l0 + BLK)))
            g.remote_dma_fused(tr, local_sem=T.sem.snt)
            sent[0] += len(on_eng) + len(off_eng)
        n_near, n_far = 2 * half + len(on_eng), 4 * half
        for kind in "CS":
            for far in (False, True):
                views = []
                for s in (me["fx"] + me["fy"] if far else me["near"] + [me["peer"]]):
                    st, l0 = landing(L, x, s, rank)
                    views.append(v(st + kind, l0, l0 + BLK))
                total = n_near + n_far if x % 2 == 0 else 2 * (n_far if far else n_near)
                after("R", [], views, (arrival_sem(x, kind, far), total, {}))

    far0, near0 = BLK * kfar, BLK * (4 - kfar)

    def unpack(b0, stem, c0, first):
        for b in range(4):
            mm(b0 + b, "u", 128 * b, stem, c0, HALF, first, not first)

    def blend(r, b0, c0):
        unpack(b0, "rt%d" % r, me["land"] + c0, False)
        for b in range(4):
            o = v("bl%d" % r, 4 * c0 + b, 4 * (c0 + HALF), 4)
            if b % 2 == 1:
                ts(o, bank(b0 + b, HALF), 0.5, ALU.mult)
            else:
                scopy(o, bank(b0 + b, HALF), 0.5)
        quant("w%d" % r, XW + c0, XW + c0 + HALF, v("bl%d" % r, 4 * c0, 4 * (c0 + HALF)))

    def drawn(k):
        if k >= 2:
            quant("x1", XS * (k - 1), XS * k, v("xt", 4 * XS * (k - 1), 4 * XS * k))

    def picker(dst, stride, src, width, lst, cuts):
        def make(k):
            if k < 2:
                pick(dst, stride * k, src, width, lst, cuts[2 * k], cuts[2 * k + 1])
        return make

    quant("x1", 0, XS, v("xt", 0, 4 * XS))
    quant("e", 0, 256, v("et", 0, 1024))
    quant("e", 256, 512, v("et", 1024, 2048))
    copy(v("au", 0, 32), v("pai", 0, 32))
    copy(v("bu", 0, 32), v("pbi", 0, 32))
    sfar = so.index(me["fx"][0]) // 4 * 4
    qf, qn = so[sfar] // 2, so[4 - sfar] // 2
    assert qf // 2 == qn // 2 and so[sfar + 2] // 2 == qf ^ 2 and so[6 - sfar] // 2 == qn ^ 2
    for r in (1, 2):
        X, D = "x%d" % r, "da" if r == 1 else "db"
        ex, sl, rt, w = ["%s%d" % (n, r) for n in ("ex", "sl", "rt", "w")]
        decode(D, X, XS, False, drawn if r == 1 else picker(X, XS, "w1", XW + ALL, "lr1", (0, 9, 10, 28)), r == 1)
        slot_list(D)
        exchange(2 * r - 2, ex, 0, fo, X, XW, "lf%d" % r)
        dma("Y", wire(T, w + "C", 0, XW), wire(T, X + "C", 0, XW), [v(X + "C", 0, XW)], [v(w + "C", 0, XW)])
        dma("Y", wire(T, w + "S", 0, XW), wire(T, X + "S", 0, XW), [v(X + "S", 0, XW)], [v(w + "S", 0, XW)])
        if r == 1:
            later_constants()
        else:
            gath_s(D, H2, A1, "au", 0, 512)
            gath_s(D, H1, A0, "au", 0, 512)
            home_list("lr2", (0, 8, 16))
        unpack(4, ex, far0, True)
        decode("da", sl, 128, True, picker(sl, 128, ex, 2 * ALL, "ls", (0, 8, 8, 24)), False)
        unpack(0, ex, near0, True)
        back("da", "inP")
        spread("inP", qf // 2, ((qf % 2, sfar), (qn % 2, 4 - sfar)))
        exchange(2 * r - 1, rt, me["send"], so, "e", S, "lp%d" % r)
        if r == 1:
            home_list("lr1", (0, 10, 19))
        else:
            back(D, "inH")
            dma("Y", T.ol[:], T.inH[:, 0:3], [v("inH", 0, 3)], [])
            dma("Y", T.dl[:], T.inP[:, 0:3], [v("inP", 0, 3)], [])
        blend(r, 0, near0)
        blend(r, 4, far0)

    for t in range(TT):
        pick("x3", 128 * t, "w2", XW + ALL, "lr2", 8 * t, 8 * t + 8)
        mm(t, "v", 0, "x3", 128 * t, 128)
    for a, b in ((0, 256), (256, ALL)):
        dma("Y", T.oc[:, 4 * a:4 * b], wire(T, "x3C", a, b), [v("x3C", a, b)], [])
    for k in range(4):
        dma("S", T.osc[4 * k:4 * k + 4, :], T.x3S[32 * k:32 * k + 4, :], [v("x3S", 0, ALL)], [])
    for t in range(TT):
        copy(v("yt", 128 * t, 128 * t + 128), bank(t, 128))
    for a, b in ((0, 256), (256, ALL)):
        dma("Y", T.y[:, a:b], T.yt[:, a:b], [v("yt", a, b)], [])
    g.wait_ge(T.sem.snt, sent[0])
    for s in final:
        if waited.get(s, 0) < final[s]:
            g.wait_ge(T.sem[s], final[s])
